import numpy as np
import ml_dtypes

BF16 = ml_dtypes.bfloat16


def bf(x):
    return np.asarray(x, np.float32).astype(BF16)


def f32(x):
    return np.asarray(x, np.float32)


def f64(x):
    return np.asarray(x).astype(np.float64)


def striped(idx):
    return np.tile(idx.reshape(-1, 16).T, (8, 1))


S, K, M, N, D, V = 512, 128, 256, 384, 2, 192


def setup_inputs():
    return {"table": bf(np.random.standard_normal((S, K))), "w": bf(np.random.standard_normal((D, K, M)) / np.sqrt(D * K)), "r": f32(np.random.standard_normal((M, V))), "offs": striped(np.random.permutation(np.tile(np.arange(S), 2))[:N])}


def reference(table, w, r, offs):
    idx = offs[:16].T.reshape(-1)
    x = f64(table)[idx].T
    y = sum(f64(w)[t].T @ x[:, t * V : (t + 1) * V] for t in range(D))
    return y + f64(r)

@@ -1,0 +1,56 @@
+import concourse.mybir as mybir
+from concourse.masks import make_identity
+
+BF16, F32, U16 = mybir.dt.bfloat16, mybir.dt.float32, mybir.dt.uint16
+
+P = 128
+NODES = 512
+FEATURES = 128
+OUT_FEATURES = 256
+EDGES = 192
+ENDS = 2
+NODE_BLOCKS = NODES // P
+OUT_BLOCKS = OUT_FEATURES // P
+LIST_COLUMNS = EDGES // 16
+
+FLOPS = 2 * FEATURES * OUT_FEATURES * ENDS * EDGES
+
+
+def tile_gather_matmul_kernel(tc, table, w, r, offs, out):
+    nc = tc.nc
+    with (
+        tc.tile_pool(name="held", bufs=1) as held,
+        tc.psum_pool(name="flip", bufs=1) as flip,
+        tc.psum_pool(name="sums", bufs=1) as sums,
+    ):
+        offsets = held.tile([P, ENDS * LIST_COLUMNS], U16, name="offsets")
+        nc.sync.dma_start(offsets[:], offs)
+        node_rows = held.tile([P, NODE_BLOCKS, FEATURES], BF16, name="node_rows")
+        nc.scalar.dma_start(node_rows[:], table.rearrange("(a p) k -> p a k", p=P))
+        weights = held.tile([P, ENDS, OUT_FEATURES], BF16, name="weights")
+        nc.sync.dma_start(weights[:], w.rearrange("t k m -> k t m"))
+        edge_terms = held.tile([P, OUT_BLOCKS, EDGES], F32, name="edge_terms")
+        nc.sync.dma_start(edge_terms[:], r.rearrange("(b p) v -> p b v", p=P))
+
+        identity = held.tile([P, P], BF16, name="identity")
+        make_identity(nc, identity[:])
+        flipped = flip.tile([P, NODES], BF16, name="flipped")
+        for a in range(NODE_BLOCKS):
+            nc.tensor.transpose(flipped[:, a * P : (a + 1) * P], node_rows[:, a, :], identity[:])
+        window = held.tile([P, NODES], BF16, name="window")
+        nc.vector.tensor_copy(window[:], flipped[:])
+
+        for b in range(OUT_BLOCKS):
+            bank = sums.tile([P, EDGES], F32, name=f"bank{b}")
+            for t in range(ENDS):
+                picked = window[:].indirect(offsets[:, t * LIST_COLUMNS : (t + 1) * LIST_COLUMNS])
+                nc.tensor.matmul(
+                    bank[:],
+                    weights[:, t, b * P : (b + 1) * P],
+                    picked,
+                    start=(t == 0),
+                    stop=(t == ENDS - 1),
+                )
+            result = held.tile([P, EDGES], F32, name=f"result{b}")
+            nc.vector.tensor_tensor(result[:], bank[:], edge_terms[:, b, :], mybir.AluOpType.add)
+            nc.sync.dma_start(out[b * P : (b + 1) * P, :], result[:])

@@ -25,21 +25,24 @@ def tile_gather_matmul_kernel(tc, table, w, r, offs, out):
     ):
         offsets = held.tile([P, ENDS * LIST_COLUMNS], U16, name="offsets")
         nc.sync.dma_start(offsets[:], offs)
-        node_rows = held.tile([P, NODE_BLOCKS, FEATURES], BF16, name="node_rows")
-        nc.scalar.dma_start(node_rows[:], table.rearrange("(a p) k -> p a k", p=P))
+        node_rows = [held.tile([P, FEATURES], BF16, name=f"node_rows{a}") for a in range(NODE_BLOCKS)]
+        for a in range(NODE_BLOCKS):
+            nc.sync.dma_start(node_rows[a][:], table[a * P : (a + 1) * P, :])
         weights = held.tile([P, ENDS, OUT_FEATURES], BF16, name="weights")
         nc.sync.dma_start(weights[:], w.rearrange("t k m -> k t m"))
-        edge_terms = held.tile([P, OUT_BLOCKS, EDGES], F32, name="edge_terms")
-        nc.sync.dma_start(edge_terms[:], r.rearrange("(b p) v -> p b v", p=P))
 
         identity = held.tile([P, P], BF16, name="identity")
         make_identity(nc, identity[:])
-        flipped = flip.tile([P, NODES], BF16, name="flipped")
-        for a in range(NODE_BLOCKS):
-            nc.tensor.transpose(flipped[:, a * P : (a + 1) * P], node_rows[:, a, :], identity[:])
-        window = held.tile([P, NODES], BF16, name="window")
-        nc.vector.tensor_copy(window[:], flipped[:])
+        edge_terms = held.tile([P, OUT_BLOCKS, EDGES], F32, name="edge_terms")
+        nc.gpsimd.dma_start(edge_terms[:], r.rearrange("(b p) v -> p b v", p=P))
 
+        window = held.tile([P, NODES], BF16, name="window")
+        for a in range(NODE_BLOCKS):
+            flipped = flip.tile([P, P], BF16, name=f"flipped{a}")
+            nc.tensor.transpose(flipped[:], node_rows[a][:], identity[:])
+            nc.vector.tensor_copy(window[:, a * P : (a + 1) * P], flipped[:])
+
+        store_queues = [nc.sync, nc.scalar]
         for b in range(OUT_BLOCKS):
             bank = sums.tile([P, EDGES], F32, name=f"bank{b}")
             for t in range(ENDS):
@@ -53,4 +56,4 @@ def tile_gather_matmul_kernel(tc, table, w, r, offs, out):
                 )
             result = held.tile([P, EDGES], F32, name=f"result{b}")
             nc.vector.tensor_tensor(result[:], bank[:], edge_terms[:, b, :], mybir.AluOpType.add)
-            nc.sync.dma_start(out[b * P : (b + 1) * P, :], result[:])
+            store_queues[b].dma_start(out[b * P : (b + 1) * P, :], result[:])

@@ -23,26 +23,24 @@ def tile_gather_matmul_kernel(tc, table, w, r, offs, out):
         tc.psum_pool(name="flip", bufs=1) as flip,
         tc.psum_pool(name="sums", bufs=1) as sums,
     ):
-        offsets = held.tile([P, ENDS * LIST_COLUMNS], U16, name="offsets")
-        nc.sync.dma_start(offsets[:], offs)
         node_rows = [held.tile([P, FEATURES], BF16, name=f"node_rows{a}") for a in range(NODE_BLOCKS)]
         for a in range(NODE_BLOCKS):
-            nc.sync.dma_start(node_rows[a][:], table[a * P : (a + 1) * P, :])
+            nc.scalar.dma_start(node_rows[a][:], table[a * P : (a + 1) * P, :])
+        offsets = held.tile([P, ENDS * LIST_COLUMNS], U16, name="offsets")
+        nc.sync.dma_start(offsets[:], offs)
         weights = held.tile([P, ENDS, OUT_FEATURES], BF16, name="weights")
         nc.sync.dma_start(weights[:], w.rearrange("t k m -> k t m"))
+        edge_terms = held.tile([P, OUT_BLOCKS, EDGES], F32, name="edge_terms")
+        nc.sync.dma_start(edge_terms[:], r.rearrange("(b p) v -> p b v", p=P))
 
         identity = held.tile([P, P], BF16, name="identity")
         make_identity(nc, identity[:])
-        edge_terms = held.tile([P, OUT_BLOCKS, EDGES], F32, name="edge_terms")
-        nc.gpsimd.dma_start(edge_terms[:], r.rearrange("(b p) v -> p b v", p=P))
-
         window = held.tile([P, NODES], BF16, name="window")
         for a in range(NODE_BLOCKS):
             flipped = flip.tile([P, P], BF16, name=f"flipped{a}")
             nc.tensor.transpose(flipped[:], node_rows[a][:], identity[:])
             nc.vector.tensor_copy(window[:, a * P : (a + 1) * P], flipped[:])
 
-        store_queues = [nc.sync, nc.scalar]
         for b in range(OUT_BLOCKS):
             bank = sums.tile([P, EDGES], F32, name=f"bank{b}")
             for t in range(ENDS):
@@ -56,4 +54,4 @@ def tile_gather_matmul_kernel(tc, table, w, r, offs, out):
                 )
             result = held.tile([P, EDGES], F32, name=f"result{b}")
             nc.vector.tensor_tensor(result[:], bank[:], edge_terms[:, b, :], mybir.AluOpType.add)
-            store_queues[b].dma_start(out[b * P : (b + 1) * P, :], result[:])
+            nc.sync.dma_start(out[b * P : (b + 1) * P, :], result[:])

@@ -12,6 +12,8 @@ ENDS = 2
 NODE_BLOCKS = NODES // P
 OUT_BLOCKS = OUT_FEATURES // P
 LIST_COLUMNS = EDGES // 16
+BANK_COLUMNS = 512
+WARM_UP_MATMULS = 2 * 1024 // BANK_COLUMNS
 
 FLOPS = 2 * FEATURES * OUT_FEATURES * ENDS * EDGES
 
@@ -22,12 +24,18 @@ def tile_gather_matmul_kernel(tc, table, w, r, offs, out):
         tc.tile_pool(name="held", bufs=1) as held,
         tc.psum_pool(name="flip", bufs=1) as flip,
         tc.psum_pool(name="sums", bufs=1) as sums,
+        tc.psum_pool(name="idle", bufs=1) as idle,
     ):
-        node_rows = [held.tile([P, FEATURES], BF16, name=f"node_rows{a}") for a in range(NODE_BLOCKS)]
-        for a in range(NODE_BLOCKS):
-            nc.scalar.dma_start(node_rows[a][:], table[a * P : (a + 1) * P, :])
+        zeros = held.tile([P, BANK_COLUMNS], BF16, name="zeros")
+        nc.vector.memset(zeros[:], 0.0)
+        unread = idle.tile([P, BANK_COLUMNS], F32, name="unread")
+        for repeat in range(WARM_UP_MATMULS):
+            nc.tensor.matmul(unread[:], zeros[:, :P], zeros[:], start=True, stop=True)
+
         offsets = held.tile([P, ENDS * LIST_COLUMNS], U16, name="offsets")
         nc.sync.dma_start(offsets[:], offs)
+        node_rows = held.tile([P, NODE_BLOCKS, FEATURES], BF16, name="node_rows")
+        nc.scalar.dma_start(node_rows[:], table.rearrange("(a p) k -> p a k", p=P))
         weights = held.tile([P, ENDS, OUT_FEATURES], BF16, name="weights")
         nc.sync.dma_start(weights[:], w.rearrange("t k m -> k t m"))
         edge_terms = held.tile([P, OUT_BLOCKS, EDGES], F32, name="edge_terms")
@@ -35,11 +43,11 @@ def tile_gather_matmul_kernel(tc, table, w, r, offs, out):
 
         identity = held.tile([P, P], BF16, name="identity")
         make_identity(nc, identity[:])
-        window = held.tile([P, NODES], BF16, name="window")
+        flipped = flip.tile([P, NODES], BF16, name="flipped")
         for a in range(NODE_BLOCKS):
-            flipped = flip.tile([P, P], BF16, name=f"flipped{a}")
-            nc.tensor.transpose(flipped[:], node_rows[a][:], identity[:])
-            nc.vector.tensor_copy(window[:, a * P : (a + 1) * P], flipped[:])
+            nc.tensor.transpose(flipped[:, a * P : (a + 1) * P], node_rows[:, a, :], identity[:])
+        window = held.tile([P, NODES], BF16, name="window")
+        nc.vector.tensor_copy(window[:], flipped[:])
 
         for b in range(OUT_BLOCKS):
             bank = sums.tile([P, EDGES], F32, name=f"bank{b}")

@@ -12,8 +12,6 @@ ENDS = 2
 NODE_BLOCKS = NODES // P
 OUT_BLOCKS = OUT_FEATURES // P
 LIST_COLUMNS = EDGES // 16
-BANK_COLUMNS = 512
-WARM_UP_MATMULS = 2 * 1024 // BANK_COLUMNS
 
 FLOPS = 2 * FEATURES * OUT_FEATURES * ENDS * EDGES
 
@@ -24,18 +22,11 @@ def tile_gather_matmul_kernel(tc, table, w, r, offs, out):
         tc.tile_pool(name="held", bufs=1) as held,
         tc.psum_pool(name="flip", bufs=1) as flip,
         tc.psum_pool(name="sums", bufs=1) as sums,
-        tc.psum_pool(name="idle", bufs=1) as idle,
     ):
-        zeros = held.tile([P, BANK_COLUMNS], BF16, name="zeros")
-        nc.vector.memset(zeros[:], 0.0)
-        unread = idle.tile([P, BANK_COLUMNS], F32, name="unread")
-        for repeat in range(WARM_UP_MATMULS):
-            nc.tensor.matmul(unread[:], zeros[:, :P], zeros[:], start=True, stop=True)
-
+        node_rows = held.tile([P, NODE_BLOCKS, FEATURES], BF16, name="node_rows")
+        nc.sync.dma_start(node_rows[:], table.rearrange("(a p) k -> p a k", p=P))
         offsets = held.tile([P, ENDS * LIST_COLUMNS], U16, name="offsets")
         nc.sync.dma_start(offsets[:], offs)
-        node_rows = held.tile([P, NODE_BLOCKS, FEATURES], BF16, name="node_rows")
-        nc.scalar.dma_start(node_rows[:], table.rearrange("(a p) k -> p a k", p=P))
         weights = held.tile([P, ENDS, OUT_FEATURES], BF16, name="weights")
         nc.sync.dma_start(weights[:], w.rearrange("t k m -> k t m"))
         edge_terms = held.tile([P, OUT_BLOCKS, EDGES], F32, name="edge_terms")

@@ -13,6 +13,9 @@ NODE_BLOCKS = NODES // P
 OUT_BLOCKS = OUT_FEATURES // P
 LIST_COLUMNS = EDGES // 16
 
+FLIP_BANKS = 2
+BLOCKS_A_BANK = NODE_BLOCKS // FLIP_BANKS
+
 FLOPS = 2 * FEATURES * OUT_FEATURES * ENDS * EDGES
 
 
@@ -34,11 +37,12 @@ def tile_gather_matmul_kernel(tc, table, w, r, offs, out):
 
         identity = held.tile([P, P], BF16, name="identity")
         make_identity(nc, identity[:])
-        flipped = flip.tile([P, NODES], BF16, name="flipped")
-        for a in range(NODE_BLOCKS):
-            nc.tensor.transpose(flipped[:, a * P : (a + 1) * P], node_rows[:, a, :], identity[:])
         window = held.tile([P, NODES], BF16, name="window")
-        nc.vector.tensor_copy(window[:], flipped[:])
+        for h in range(FLIP_BANKS):
+            flipped = flip.tile([P, BLOCKS_A_BANK * P], BF16, name=f"flipped{h}")
+            for j in range(BLOCKS_A_BANK):
+                nc.tensor.transpose(flipped[:, j * P : (j + 1) * P], node_rows[:, h * BLOCKS_A_BANK + j, :], identity[:])
+            nc.vector.tensor_copy(window[:, h * BLOCKS_A_BANK * P : (h + 1) * BLOCKS_A_BANK * P], flipped[:])
 
         for b in range(OUT_BLOCKS):
             bank = sums.tile([P, EDGES], F32, name=f"bank{b}")

@@ -13,7 +13,7 @@ NODE_BLOCKS = NODES // P
 OUT_BLOCKS = OUT_FEATURES // P
 LIST_COLUMNS = EDGES // 16
 
-FLIP_BANKS = 2
+FLIP_BANKS = 4
 BLOCKS_A_BANK = NODE_BLOCKS // FLIP_BANKS
 
 FLOPS = 2 * FEATURES * OUT_FEATURES * ENDS * EDGES

@@ -16,6 +16,8 @@ LIST_COLUMNS = EDGES // 16
 FLIP_BANKS = 4
 BLOCKS_A_BANK = NODE_BLOCKS // FLIP_BANKS
 
+BLOCKS_A_LOAD = 2
+
 FLOPS = 2 * FEATURES * OUT_FEATURES * ENDS * EDGES
 
 
@@ -27,7 +29,12 @@ def tile_gather_matmul_kernel(tc, table, w, r, offs, out):
         tc.psum_pool(name="sums", bufs=1) as sums,
     ):
         node_rows = held.tile([P, NODE_BLOCKS, FEATURES], BF16, name="node_rows")
-        nc.sync.dma_start(node_rows[:], table.rearrange("(a p) k -> p a k", p=P))
+        blocks_of_rows = table.rearrange("(a p) k -> p a k", p=P)
+        for first in range(0, NODE_BLOCKS, BLOCKS_A_LOAD):
+            nc.sync.dma_start(
+                node_rows[:, first : first + BLOCKS_A_LOAD, :],
+                blocks_of_rows[:, first : first + BLOCKS_A_LOAD, :],
+            )
         offsets = held.tile([P, ENDS * LIST_COLUMNS], U16, name="offsets")
         nc.sync.dma_start(offsets[:], offs)
         weights = held.tile([P, ENDS, OUT_FEATURES], BF16, name="weights")

@@ -38,7 +38,9 @@ def tile_gather_matmul_kernel(tc, table, w, r, offs, out):
         offsets = held.tile([P, ENDS * LIST_COLUMNS], U16, name="offsets")
         nc.sync.dma_start(offsets[:], offs)
         weights = held.tile([P, ENDS, OUT_FEATURES], BF16, name="weights")
-        nc.sync.dma_start(weights[:], w.rearrange("t k m -> k t m"))
+        features_first = w.rearrange("t k m -> k t m")
+        for b in range(OUT_BLOCKS):
+            nc.sync.dma_start(weights[:, :, b * P : (b + 1) * P], features_first[:, :, b * P : (b + 1) * P])
         edge_terms = held.tile([P, OUT_BLOCKS, EDGES], F32, name="edge_terms")
         nc.sync.dma_start(edge_terms[:], r.rearrange("(b p) v -> p b v", p=P))
 

@@ -18,6 +18,9 @@ BLOCKS_A_BANK = NODE_BLOCKS // FLIP_BANKS
 
 BLOCKS_A_LOAD = 2
 
+WARM_COLUMNS = 512
+WARM_MATMULS = 3
+
 FLOPS = 2 * FEATURES * OUT_FEATURES * ENDS * EDGES
 
 
@@ -28,6 +31,13 @@ def tile_gather_matmul_kernel(tc, table, w, r, offs, out):
         tc.psum_pool(name="flip", bufs=1) as flip,
         tc.psum_pool(name="sums", bufs=1) as sums,
     ):
+        zero_words = held.tile([P, WARM_COLUMNS // 2], F32, name="zero_words")
+        nc.gpsimd.memset(zero_words[:], 0.0)
+        zeros = zero_words[:].bitcast(BF16)
+        unread = sums.tile([P, WARM_COLUMNS], F32, name="unread")
+        for i in range(WARM_MATMULS):
+            nc.tensor.matmul(unread[:], zeros[:, :P], zeros, start=True, stop=True)
+
         node_rows = held.tile([P, NODE_BLOCKS, FEATURES], BF16, name="node_rows")
         blocks_of_rows = table.rearrange("(a p) k -> p a k", p=P)
         for first in range(0, NODE_BLOCKS, BLOCKS_A_LOAD):

import concourse.mybir as mybir
from concourse.masks import make_identity

BF16, F32, U16 = mybir.dt.bfloat16, mybir.dt.float32, mybir.dt.uint16

P = 128
NODES = 512
FEATURES = 128
OUT_FEATURES = 256
EDGES = 192
ENDS = 2
NODE_BLOCKS = NODES // P
OUT_BLOCKS = OUT_FEATURES // P
LIST_COLUMNS = EDGES // 16

FLIP_BANKS = 4
BLOCKS_A_BANK = NODE_BLOCKS // FLIP_BANKS

BLOCKS_A_LOAD = 2

WARM_COLUMNS = 512
WARM_MATMULS = 3

FLOPS = 2 * FEATURES * OUT_FEATURES * ENDS * EDGES


def tile_gather_matmul_kernel(tc, table, w, r, offs, out):
    nc = tc.nc
    with (
        tc.tile_pool(name="held", bufs=1) as held,
        tc.psum_pool(name="flip", bufs=1) as flip,
        tc.psum_pool(name="sums", bufs=1) as sums,
    ):
        zero_words = held.tile([P, WARM_COLUMNS // 2], F32, name="zero_words")
        nc.gpsimd.memset(zero_words[:], 0.0)
        zeros = zero_words[:].bitcast(BF16)
        unread = sums.tile([P, WARM_COLUMNS], F32, name="unread")
        for i in range(WARM_MATMULS):
            nc.tensor.matmul(unread[:], zeros[:, :P], zeros, start=True, stop=True)

        node_rows = held.tile([P, NODE_BLOCKS, FEATURES], BF16, name="node_rows")
        blocks_of_rows = table.rearrange("(a p) k -> p a k", p=P)
        for first in range(0, NODE_BLOCKS, BLOCKS_A_LOAD):
            nc.sync.dma_start(
                node_rows[:, first : first + BLOCKS_A_LOAD, :],
                blocks_of_rows[:, first : first + BLOCKS_A_LOAD, :],
            )
        offsets = held.tile([P, ENDS * LIST_COLUMNS], U16, name="offsets")
        nc.sync.dma_start(offsets[:], offs)
        weights = held.tile([P, ENDS, OUT_FEATURES], BF16, name="weights")
        features_first = w.rearrange("t k m -> k t m")
        for b in range(OUT_BLOCKS):
            nc.sync.dma_start(weights[:, :, b * P : (b + 1) * P], features_first[:, :, b * P : (b + 1) * P])
        edge_terms = held.tile([P, OUT_BLOCKS, EDGES], F32, name="edge_terms")
        nc.sync.dma_start(edge_terms[:], r.rearrange("(b p) v -> p b v", p=P))

        identity = held.tile([P, P], BF16, name="identity")
        make_identity(nc, identity[:])
        window = held.tile([P, NODES], BF16, name="window")
        for h in range(FLIP_BANKS):
            flipped = flip.tile([P, BLOCKS_A_BANK * P], BF16, name=f"flipped{h}")
            for j in range(BLOCKS_A_BANK):
                nc.tensor.transpose(flipped[:, j * P : (j + 1) * P], node_rows[:, h * BLOCKS_A_BANK + j, :], identity[:])
            nc.vector.tensor_copy(window[:, h * BLOCKS_A_BANK * P : (h + 1) * BLOCKS_A_BANK * P], flipped[:])

        for b in range(OUT_BLOCKS):
            bank = sums.tile([P, EDGES], F32, name=f"bank{b}")
            for t in range(ENDS):
                picked = window[:].indirect(offsets[:, t * LIST_COLUMNS : (t + 1) * LIST_COLUMNS])
                nc.tensor.matmul(
                    bank[:],
                    weights[:, t, b * P : (b + 1) * P],
                    picked,
                    start=(t == 0),
                    stop=(t == ENDS - 1),
                )
            result = held.tile([P, EDGES], F32, name=f"result{b}")
            nc.vector.tensor_tensor(result[:], bank[:], edge_terms[:, b, :], mybir.AluOpType.add)
            nc.sync.dma_start(out[b * P : (b + 1) * P, :], result[:])
